import numpy as np, ml_dtypes
CORES = [35,38,43,46]
N = 4
R, TK = 32, 128
WID = [16,16,128,80]
def setup_inputs(rng):
    u = (rng.standard_normal((N, 128, R), dtype=np.float32) / 11).astype(ml_dtypes.bfloat16)
    return {"x": rng.standard_normal((N, 128, TK), dtype=np.float32).astype(ml_dtypes.bfloat16), "u": u, "ut": u.transpose(0, 2, 1).copy(), "vt": rng.standard_normal((N, R, 128), dtype=np.float32).astype(ml_dtypes.bfloat16)}
def setup_inputs_big(rng):
    d = setup_inputs(rng)
    for k in ("x", "u", "ut", "vt"): d[k] = (d[k].astype(np.float32) * 1024.0).astype(d[k].dtype)
    return d
def setup_inputs_small(rng):
    d = setup_inputs(rng)
    for k in ("x", "u", "ut", "vt"): d[k] = (d[k].astype(np.float32) * (1 / 1024.0)).astype(d[k].dtype)
    return d
def setup_inputs_apart(rng):
    d = setup_inputs(rng)
    f = (10.0 ** rng.permutation(np.linspace(-1.5, 1.5, N))).astype(np.float32).reshape(N, 1, 1)
    for k in ("x", "u", "ut", "vt"): d[k] = (d[k].astype(np.float32) * f).astype(d[k].dtype)
    return d
def tie_inputs(x):
    x = dict(x)
    x["ut"] = x["u"].transpose(0, 2, 1).copy()
    return x
def whole(x, u, ut, vt):
    X, U, VT = x.astype(np.float64), u.astype(np.float64), vt.astype(np.float64)
    y = np.stack([sum(VT[j].T @ (U[j].T @ X[r]) for j in range(N)) for r in range(N)])
    return {"y": y.astype(ml_dtypes.bfloat16 if x.dtype != np.float64 else np.float64)}
def reference(x, u, ut, vt):
    o = whole(x, u, ut, vt)["y"].copy()
    for r in range(N):
        o[r][:, WID[r]:] = np.nan
    return {"y": o}

@@ -1,0 +1,90 @@
+from concourse.bass import DstId, RemoteDMATransfer
+
+NR, RK, D = 4, 32, 128
+ENG = 1
+
+SCRATCH = {
+    "GU": ("dram", [NR, 128, RK], "bfloat16"),
+    "GV": ("dram", [NR, 128, RK], "bfloat16"),
+    "UT": ("sbuf", [128, D], "bfloat16"),
+    "VT": ("sbuf", [128, D], "bfloat16"),
+    "X": ("sbuf", [128, D], "bfloat16"),
+    "MT": ("sbuf", [128, D], "bfloat16"),
+    "Y": ("sbuf", [128, D], "bfloat16"),
+    "PM": ("psum", [128, 512], "float32"),
+    "PY": ("psum", [128, 512], "float32"),
+}
+SEMAPHORES = ["staged", "sent", "near", "far", "loaded", "xin", "mm1", "cp1", "mm2", "cp2", "stored"]
+
+
+def _bits(mask):
+    return [e for e in range(mask.bit_length()) if (mask >> e) & 1]
+
+
+def _runs(ranks):
+    out = []
+    for j in ranks:
+        if out and out[-1][0] + out[-1][1] == j:
+            out[-1] = (out[-1][0], out[-1][1] + 1)
+        else:
+            out.append((j, 1))
+    return out
+
+
+def rank_program(g, core, T, topo):
+    r = T.rank_of(core)
+    if r is None:
+        return
+    S = T.sem
+    cores = T.cores
+    W = T.tables["WID"][r]
+    others = [j for j in range(len(cores)) if j != r]
+    near = [j for j in others if topo.chip(cores[j]) == topo.chip(core)]
+    far = [j for j in others if topo.chip(cores[j]) != topo.chip(core)]
+
+    g.sync.dma_start(T.GU[r], T.ut[:]).then_inc(S.staged, 16)
+    g.scalar.dma_start(T.GV[r], T.vt[:]).then_inc(S.staged, 16)
+    g.sync.dma_start(T.UT[RK * r:RK * (r + 1), :], T.ut[:]).then_inc(S.loaded, 16)
+    g.scalar.dma_start(T.VT[RK * r:RK * (r + 1), :], T.vt[:]).then_inc(S.loaded, 16)
+    g.sync.dma_start(T.X[:, 0:W], T.x[:, 0:W]).then_inc(S.xin, 16)
+    loads = 2
+
+    used = []
+    transfers = []
+    for j in far + near:
+        dst = cores[j]
+        rid, pid, _ = topo.addr(dst)
+        sem = S.far if topo.chip(dst) != topo.chip(core) else S.near
+        for buf in (T.GU, T.GV):
+            free = [e for e in _bits(topo.mask(core, dst)) if e not in used]
+            free.sort(key=lambda e: (e % 2, e))
+            mine = free[:ENG]
+            used.extend(mine)
+            transfers.append(RemoteDMATransfer(dst_ids=[DstId(rid=rid, pnc=pid)], dma_engine_mask=sum(1 << e for e in mine),
+                                               remote_sem=sem, src=buf[r], dst=buf[r]))
+    g.wait_ge(S.staged, 32)
+    g.remote_dma_fused(transfers, local_sem=S.sent)
+
+    for group, sem in ((near, S.near), (far, S.far)):
+        if not group:
+            continue
+        g.sync.wait_ge(sem, 2 * ENG * len(group))
+        g.scalar.wait_ge(sem, 2 * ENG * len(group))
+        for a, n in _runs(group):
+            g.sync.dma_start(T.UT[RK * a:RK * (a + n), :], T.GU[a:a + n]).then_inc(S.loaded, 16)
+            g.scalar.dma_start(T.VT[RK * a:RK * (a + n), :], T.GV[a:a + n]).then_inc(S.loaded, 16)
+            loads += 2
+
+    g.tensor.wait_ge(S.loaded, 16 * loads)
+    g.tensor.matmul(T.PM[:, 0:D], T.UT[:], T.VT[:], start=True, stop=True).then_inc(S.mm1, 1)
+    g.vector.wait_ge(S.mm1, 1)
+    g.vector.tensor_copy(T.MT[:], T.PM[:, 0:D]).then_inc(S.cp1, 1)
+    g.tensor.wait_ge(S.xin, 16)
+    g.tensor.wait_ge(S.cp1, 1)
+    g.tensor.matmul(T.PY[:, 0:W], T.MT[:], T.X[:, 0:W], start=True, stop=True).then_inc(S.mm2, 1)
+    g.vector.wait_ge(S.mm2, 1)
+    g.vector.tensor_copy(T.Y[:, 0:W], T.PY[:, 0:W]).then_inc(S.cp2, 1)
+    g.sync.wait_ge(S.cp2, 1)
+    g.sync.dma_start(T.y[:, 0:W], T.Y[:, 0:W]).then_inc(S.stored, 16)
+    g.sync.wait_ge(S.stored, 16)
+    g.wait_ge(S.sent, ENG * len(transfers))

@@ -1,34 +1,22 @@
 from concourse.bass import DstId, RemoteDMATransfer
 
 NR, RK, D = 4, 32, 128
-ENG = 1
+ENG = 4
 
 SCRATCH = {
-    "GU": ("dram", [NR, 128, RK], "bfloat16"),
-    "GV": ("dram", [NR, 128, RK], "bfloat16"),
-    "UT": ("sbuf", [128, D], "bfloat16"),
-    "VT": ("sbuf", [128, D], "bfloat16"),
+    "UO": ("sbuf", [RK, D], "bfloat16"),
+    "VO": ("sbuf", [RK, D], "bfloat16"),
     "X": ("sbuf", [128, D], "bfloat16"),
-    "MT": ("sbuf", [128, D], "bfloat16"),
+    "MS": ("sbuf", [128, NR * D], "bfloat16"),
     "Y": ("sbuf", [128, D], "bfloat16"),
     "PM": ("psum", [128, 512], "float32"),
     "PY": ("psum", [128, 512], "float32"),
 }
-SEMAPHORES = ["staged", "sent", "near", "far", "loaded", "xin", "mm1", "cp1", "mm2", "cp2", "stored"]
+SEMAPHORES = ["loaded", "xin", "sent", "near", "far", "mm1", "cp1", "mm2", "cp2", "stored"]
 
 
 def _bits(mask):
     return [e for e in range(mask.bit_length()) if (mask >> e) & 1]
-
-
-def _runs(ranks):
-    out = []
-    for j in ranks:
-        if out and out[-1][0] + out[-1][1] == j:
-            out[-1] = (out[-1][0], out[-1][1] + 1)
-        else:
-            out.append((j, 1))
-    return out
 
 
 def rank_program(g, core, T, topo):
@@ -42,12 +30,17 @@ def rank_program(g, core, T, topo):
     near = [j for j in others if topo.chip(cores[j]) == topo.chip(core)]
     far = [j for j in others if topo.chip(cores[j]) != topo.chip(core)]
 
-    g.sync.dma_start(T.GU[r], T.ut[:]).then_inc(S.staged, 16)
-    g.scalar.dma_start(T.GV[r], T.vt[:]).then_inc(S.staged, 16)
-    g.sync.dma_start(T.UT[RK * r:RK * (r + 1), :], T.ut[:]).then_inc(S.loaded, 16)
-    g.scalar.dma_start(T.VT[RK * r:RK * (r + 1), :], T.vt[:]).then_inc(S.loaded, 16)
+    def slot(j):
+        return T.MS[:, D * j:D * (j + 1)]
+
+    g.sync.dma_start(T.UO[:], T.ut[:]).then_inc(S.loaded, 16)
+    g.scalar.dma_start(T.VO[:], T.vt[:]).then_inc(S.loaded, 16)
     g.sync.dma_start(T.X[:, 0:W], T.x[:, 0:W]).then_inc(S.xin, 16)
-    loads = 2
+
+    g.tensor.wait_ge(S.loaded, 32)
+    g.tensor.matmul(T.PM[:, 0:D], T.UO[:], T.VO[:], start=True, stop=True).then_inc(S.mm1, 1)
+    g.vector.wait_ge(S.mm1, 1)
+    g.vector.tensor_copy(slot(r), T.PM[:, 0:D]).then_inc(S.cp1, 1)
 
     used = []
     transfers = []
@@ -55,33 +48,23 @@ def rank_program(g, core, T, topo):
         dst = cores[j]
         rid, pid, _ = topo.addr(dst)
         sem = S.far if topo.chip(dst) != topo.chip(core) else S.near
-        for buf in (T.GU, T.GV):
-            free = [e for e in _bits(topo.mask(core, dst)) if e not in used]
-            free.sort(key=lambda e: (e % 2, e))
-            mine = free[:ENG]
-            used.extend(mine)
-            transfers.append(RemoteDMATransfer(dst_ids=[DstId(rid=rid, pnc=pid)], dma_engine_mask=sum(1 << e for e in mine),
-                                               remote_sem=sem, src=buf[r], dst=buf[r]))
-    g.wait_ge(S.staged, 32)
+        mine = [e for e in _bits(topo.mask(core, dst)) if e not in used][:ENG]
+        used.extend(mine)
+        transfers.append(RemoteDMATransfer(dst_ids=[DstId(rid=rid, pnc=pid)], dma_engine_mask=sum(1 << e for e in mine),
+                                           remote_sem=sem, src=slot(r), dst=slot(r)))
+    g.wait_ge(S.cp1, 1)
     g.remote_dma_fused(transfers, local_sem=S.sent)
 
-    for group, sem in ((near, S.near), (far, S.far)):
-        if not group:
-            continue
-        g.sync.wait_ge(sem, 2 * ENG * len(group))
-        g.scalar.wait_ge(sem, 2 * ENG * len(group))
-        for a, n in _runs(group):
-            g.sync.dma_start(T.UT[RK * a:RK * (a + n), :], T.GU[a:a + n]).then_inc(S.loaded, 16)
-            g.scalar.dma_start(T.VT[RK * a:RK * (a + n), :], T.GV[a:a + n]).then_inc(S.loaded, 16)
-            loads += 2
-
-    g.tensor.wait_ge(S.loaded, 16 * loads)
-    g.tensor.matmul(T.PM[:, 0:D], T.UT[:], T.VT[:], start=True, stop=True).then_inc(S.mm1, 1)
-    g.vector.wait_ge(S.mm1, 1)
-    g.vector.tensor_copy(T.MT[:], T.PM[:, 0:D]).then_inc(S.cp1, 1)
-    g.tensor.wait_ge(S.xin, 16)
+    order = [r] + near + far
     g.tensor.wait_ge(S.cp1, 1)
-    g.tensor.matmul(T.PY[:, 0:W], T.MT[:], T.X[:, 0:W], start=True, stop=True).then_inc(S.mm2, 1)
+    g.tensor.wait_ge(S.xin, 16)
+    for n, j in enumerate(order):
+        if near and j == near[0]:
+            g.tensor.wait_ge(S.near, ENG * len(near))
+        if far and j == far[0]:
+            g.tensor.wait_ge(S.far, ENG * len(far))
+        mm = g.tensor.matmul(T.PY[:, 0:W], slot(j), T.X[:, 0:W], start=(n == 0), stop=(n == len(order) - 1))
+    mm.then_inc(S.mm2, 1)
     g.vector.wait_ge(S.mm2, 1)
     g.vector.tensor_copy(T.Y[:, 0:W], T.PY[:, 0:W]).then_inc(S.cp2, 1)
     g.sync.wait_ge(S.cp2, 1)

@@ -1,18 +1,25 @@
 from concourse.bass import DstId, RemoteDMATransfer
 
 NR, RK, D = 4, 32, 128
+NBW = RK + D
 ENG = 4
+BLK = 64
 
 SCRATCH = {
+    "NB": ("sbuf", [128, NBW], "bfloat16"),
+    "NL": ("sbuf", [128, (NR - 1) * NBW], "bfloat16"),
     "UO": ("sbuf", [RK, D], "bfloat16"),
-    "VO": ("sbuf", [RK, D], "bfloat16"),
     "X": ("sbuf", [128, D], "bfloat16"),
     "MS": ("sbuf", [128, NR * D], "bfloat16"),
+    "PS": ("sbuf", [RK, (NR - 1) * D], "bfloat16"),
     "Y": ("sbuf", [128, D], "bfloat16"),
     "PM": ("psum", [128, 512], "float32"),
-    "PY": ("psum", [128, 512], "float32"),
+    "PP": ("psum", [128, 512], "float32"),
+    "PY0": ("psum", [128, 512], "float32"),
+    "PY1": ("psum", [128, 512], "float32"),
 }
-SEMAPHORES = ["loaded", "xin", "sent", "near", "far", "mm1", "cp1", "mm2", "cp2", "stored"]
+SEMAPHORES = ["zero", "raw", "utin", "xin", "sent", "near", "far", "mm1", "cp1", "mmp", "cpp", "mmy0", "mmy1", "cp2",
+              "stored"]
 
 
 def _bits(mask):
@@ -26,48 +33,85 @@ def rank_program(g, core, T, topo):
     S = T.sem
     cores = T.cores
     W = T.tables["WID"][r]
-    others = [j for j in range(len(cores)) if j != r]
-    near = [j for j in others if topo.chip(cores[j]) == topo.chip(core)]
-    far = [j for j in others if topo.chip(cores[j]) != topo.chip(core)]
+
+    def near_of(i):
+        return [j for j in range(len(cores)) if j != i and topo.chip(cores[j]) == topo.chip(cores[i])]
+
+    near = near_of(r)
+    far = [j for j in range(len(cores)) if topo.chip(cores[j]) != topo.chip(core)]
 
     def slot(j):
         return T.MS[:, D * j:D * (j + 1)]
 
-    g.sync.dma_start(T.UO[:], T.ut[:]).then_inc(S.loaded, 16)
-    g.scalar.dma_start(T.VO[:], T.vt[:]).then_inc(S.loaded, 16)
-    g.sync.dma_start(T.X[:, 0:W], T.x[:, 0:W]).then_inc(S.xin, 16)
+    vt_own = T.NB[0:RK, RK:NBW]
 
-    g.tensor.wait_ge(S.loaded, 32)
-    g.tensor.matmul(T.PM[:, 0:D], T.UO[:], T.VO[:], start=True, stop=True).then_inc(S.mm1, 1)
+    g.vector.memset(T.NB[RK:2 * RK, RK:NBW], 0.0).then_inc(S.zero, 1)
+    g.vector.memset(T.NB[2 * RK:128, RK:NBW], 0.0).then_inc(S.zero, 1)
+    g.sync.dma_start(T.NB[:, 0:RK], T.u[:]).then_inc(S.raw, 16)
+    g.scalar.dma_start(vt_own, T.vt[:]).then_inc(S.raw, 16)
+    g.sync.dma_start(T.UO[:], T.ut[:]).then_inc(S.utin, 16)
+    g.scalar.dma_start(T.X[:, 0:W], T.x[:, 0:W]).then_inc(S.xin, 16)
+
+    used = []
+
+    def take(dst):
+        mine = [e for e in _bits(topo.mask(core, dst)) if e not in used][:ENG]
+        used.extend(mine)
+        return sum(1 << e for e in mine)
+
+    engines = {j: take(cores[j]) for j in far + near}
+
+    g.wait_ge(S.zero, 2)
+    g.wait_ge(S.raw, 32)
+    for j in near:
+        rid, pid, _ = topo.addr(cores[j])
+        s = near_of(j).index(r)
+        g.remote_dma(T.NL[:, NBW * s:NBW * (s + 1)], T.NB[:], S.near, S.sent, pid, rid, engines[j])
+
+    g.tensor.wait_ge(S.raw, 32)
+    g.tensor.wait_ge(S.utin, 16)
+    g.tensor.matmul(T.PM[:, 0:D], T.UO[:], vt_own, start=True, stop=True).then_inc(S.mm1, 1)
     g.vector.wait_ge(S.mm1, 1)
     g.vector.tensor_copy(slot(r), T.PM[:, 0:D]).then_inc(S.cp1, 1)
 
-    used = []
     transfers = []
-    for j in far + near:
-        dst = cores[j]
-        rid, pid, _ = topo.addr(dst)
-        sem = S.far if topo.chip(dst) != topo.chip(core) else S.near
-        mine = [e for e in _bits(topo.mask(core, dst)) if e not in used][:ENG]
-        used.extend(mine)
-        transfers.append(RemoteDMATransfer(dst_ids=[DstId(rid=rid, pnc=pid)], dma_engine_mask=sum(1 << e for e in mine),
-                                           remote_sem=sem, src=slot(r), dst=slot(r)))
+    for j in far:
+        rid, pid, _ = topo.addr(cores[j])
+        transfers.append(RemoteDMATransfer(dst_ids=[DstId(rid=rid, pnc=pid)], dma_engine_mask=engines[j],
+                                           remote_sem=S.far, src=slot(r), dst=slot(r)))
     g.wait_ge(S.cp1, 1)
     g.remote_dma_fused(transfers, local_sem=S.sent)
 
-    order = [r] + near + far
+    nb = 2 if W >= 2 * BLK else 1
+    cuts = [W * b // nb for b in range(nb + 1)]
+    blocks = [(T["PY%d" % b], cuts[b], cuts[b + 1], S["mmy%d" % b]) for b in range(nb)]
+
     g.tensor.wait_ge(S.cp1, 1)
     g.tensor.wait_ge(S.xin, 16)
-    for n, j in enumerate(order):
-        if near and j == near[0]:
-            g.tensor.wait_ge(S.near, ENG * len(near))
-        if far and j == far[0]:
-            g.tensor.wait_ge(S.far, ENG * len(far))
-        mm = g.tensor.matmul(T.PY[:, 0:W], slot(j), T.X[:, 0:W], start=(n == 0), stop=(n == len(order) - 1))
-    mm.then_inc(S.mm2, 1)
-    g.vector.wait_ge(S.mm2, 1)
-    g.vector.tensor_copy(T.Y[:, 0:W], T.PY[:, 0:W]).then_inc(S.cp2, 1)
-    g.sync.wait_ge(S.cp2, 1)
+    for py, lo, hi, _ in blocks:
+        g.tensor.matmul(py[:, 0:hi - lo], slot(r), T.X[:, lo:hi], start=True, stop=False)
+    g.tensor.wait_ge(S.near, ENG * len(near))
+    for s in range(len(near)):
+        g.tensor.matmul(T.PP[0:RK, D * s:D * s + W], T.NL[:, NBW * s:NBW * s + RK], T.X[:, 0:W],
+                        start=True, stop=True).then_inc(S.mmp, 1)
+    g.vector.wait_ge(S.mmp, len(near))
+    for s in range(len(near)):
+        g.vector.tensor_copy(T.PS[:, D * s:D * s + W], T.PP[0:RK, D * s:D * s + W]).then_inc(S.cpp, 1)
+    g.tensor.wait_ge(S.far, ENG * len(far))
+    for b, (py, lo, hi, done) in enumerate(blocks):
+        for j in far:
+            g.tensor.matmul(py[:, 0:hi - lo], slot(j), T.X[:, lo:hi], start=False, stop=False)
+        if b == 0:
+            g.tensor.wait_ge(S.cpp, len(near))
+        for s in range(len(near)):
+            mm = g.tensor.matmul(py[:, 0:hi - lo], T.NL[0:RK, NBW * s + RK:NBW * (s + 1)], T.PS[:, D * s + lo:D * s + hi],
+                                 start=False, stop=(s == len(near) - 1))
+        mm.then_inc(done, 1)
+    for py, lo, hi, done in blocks:
+        g.vector.wait_ge(done, 1)
+        g.vector.tensor_copy(T.Y[:, lo:hi], py[:, 0:hi - lo]).then_inc(S.cp2, 1)
+
+    g.sync.wait_ge(S.cp2, nb)
     g.sync.dma_start(T.y[:, 0:W], T.Y[:, 0:W]).then_inc(S.stored, 16)
     g.sync.wait_ge(S.stored, 16)
-    g.wait_ge(S.sent, ENG * len(transfers))
+    g.wait_ge(S.sent, ENG * (len(near) + len(far)))

from concourse.bass import DstId, RemoteDMATransfer

NR, RK, D = 4, 32, 128
NBW = RK + D
ENG = 4
BLK = 64

SCRATCH = {
    "NB": ("sbuf", [128, NBW], "bfloat16"),
    "NL": ("sbuf", [128, (NR - 1) * NBW], "bfloat16"),
    "UO": ("sbuf", [RK, D], "bfloat16"),
    "X": ("sbuf", [128, D], "bfloat16"),
    "MS": ("sbuf", [128, NR * D], "bfloat16"),
    "PS": ("sbuf", [RK, (NR - 1) * D], "bfloat16"),
    "Y": ("sbuf", [128, D], "bfloat16"),
    "PM": ("psum", [128, 512], "float32"),
    "PP": ("psum", [128, 512], "float32"),
    "PY0": ("psum", [128, 512], "float32"),
    "PY1": ("psum", [128, 512], "float32"),
}
SEMAPHORES = ["zero", "raw", "utin", "xin", "sent", "near", "far", "mm1", "cp1", "mmp", "cpp", "mmy0", "mmy1", "cp2",
              "stored"]


def _bits(mask):
    return [e for e in range(mask.bit_length()) if (mask >> e) & 1]


def rank_program(g, core, T, topo):
    r = T.rank_of(core)
    if r is None:
        return
    S = T.sem
    cores = T.cores
    W = T.tables["WID"][r]

    def near_of(i):
        return [j for j in range(len(cores)) if j != i and topo.chip(cores[j]) == topo.chip(cores[i])]

    near = near_of(r)
    far = [j for j in range(len(cores)) if topo.chip(cores[j]) != topo.chip(core)]

    def slot(j):
        return T.MS[:, D * j:D * (j + 1)]

    vt_own = T.NB[0:RK, RK:NBW]

    g.vector.memset(T.NB[RK:2 * RK, RK:NBW], 0.0).then_inc(S.zero, 1)
    g.vector.memset(T.NB[2 * RK:128, RK:NBW], 0.0).then_inc(S.zero, 1)
    g.sync.dma_start(T.NB[:, 0:RK], T.u[:]).then_inc(S.raw, 16)
    g.scalar.dma_start(vt_own, T.vt[:]).then_inc(S.raw, 16)
    g.sync.dma_start(T.UO[:], T.ut[:]).then_inc(S.utin, 16)
    g.scalar.dma_start(T.X[:, 0:W], T.x[:, 0:W]).then_inc(S.xin, 16)

    used = []

    def take(dst):
        mine = [e for e in _bits(topo.mask(core, dst)) if e not in used][:ENG]
        used.extend(mine)
        return sum(1 << e for e in mine)

    engines = {j: take(cores[j]) for j in far + near}

    g.wait_ge(S.zero, 2)
    g.wait_ge(S.raw, 32)
    for j in near:
        rid, pid, _ = topo.addr(cores[j])
        s = near_of(j).index(r)
        g.remote_dma(T.NL[:, NBW * s:NBW * (s + 1)], T.NB[:], S.near, S.sent, pid, rid, engines[j])

    g.tensor.wait_ge(S.raw, 32)
    g.tensor.wait_ge(S.utin, 16)
    g.tensor.matmul(T.PM[:, 0:D], T.UO[:], vt_own, start=True, stop=True).then_inc(S.mm1, 1)
    g.vector.wait_ge(S.mm1, 1)
    g.vector.tensor_copy(slot(r), T.PM[:, 0:D]).then_inc(S.cp1, 1)

    transfers = []
    for j in far:
        rid, pid, _ = topo.addr(cores[j])
        transfers.append(RemoteDMATransfer(dst_ids=[DstId(rid=rid, pnc=pid)], dma_engine_mask=engines[j],
                                           remote_sem=S.far, src=slot(r), dst=slot(r)))
    g.wait_ge(S.cp1, 1)
    g.remote_dma_fused(transfers, local_sem=S.sent)

    nb = 2 if W >= 2 * BLK else 1
    cuts = [W * b // nb for b in range(nb + 1)]
    blocks = [(T["PY%d" % b], cuts[b], cuts[b + 1], S["mmy%d" % b]) for b in range(nb)]

    g.tensor.wait_ge(S.cp1, 1)
    g.tensor.wait_ge(S.xin, 16)
    for py, lo, hi, _ in blocks:
        g.tensor.matmul(py[:, 0:hi - lo], slot(r), T.X[:, lo:hi], start=True, stop=False)
    g.tensor.wait_ge(S.near, ENG * len(near))
    for s in range(len(near)):
        g.tensor.matmul(T.PP[0:RK, D * s:D * s + W], T.NL[:, NBW * s:NBW * s + RK], T.X[:, 0:W],
                        start=True, stop=True).then_inc(S.mmp, 1)
    g.vector.wait_ge(S.mmp, len(near))
    for s in range(len(near)):
        g.vector.tensor_copy(T.PS[:, D * s:D * s + W], T.PP[0:RK, D * s:D * s + W]).then_inc(S.cpp, 1)
    g.tensor.wait_ge(S.far, ENG * len(far))
    for b, (py, lo, hi, done) in enumerate(blocks):
        for j in far:
            g.tensor.matmul(py[:, 0:hi - lo], slot(j), T.X[:, lo:hi], start=False, stop=False)
        if b == 0:
            g.tensor.wait_ge(S.cpp, len(near))
        for s in range(len(near)):
            mm = g.tensor.matmul(py[:, 0:hi - lo], T.NL[0:RK, NBW * s + RK:NBW * (s + 1)], T.PS[:, D * s + lo:D * s + hi],
                                 start=False, stop=(s == len(near) - 1))
        mm.then_inc(done, 1)
    for py, lo, hi, done in blocks:
        g.vector.wait_ge(done, 1)
        g.vector.tensor_copy(T.Y[:, lo:hi], py[:, 0:hi - lo]).then_inc(S.cp2, 1)

    g.sync.wait_ge(S.cp2, nb)
    g.sync.dma_start(T.y[:, 0:W], T.Y[:, 0:W]).then_inc(S.stored, 16)
    g.sync.wait_ge(S.stored, 16)
    g.wait_ge(S.sent, ENG * (len(near) + len(far)))
